import numpy as np
CORES = [2,10,18,26,34,42,50,58]
N = 8
WIDTHS = [128,8,40,16,64,24,4,28]
OFF = [0,128,136,176,192,256,280,284]
C = 312
def setup_inputs(rng):
    return {"x": rng.standard_normal((N, 128, C), dtype=np.float32)}
def reference(x):
    s = x.sum(axis=0, dtype=np.float64).astype(x.dtype)
    YW = max(WIDTHS)
    y = np.full((N, 128, YW), np.nan, x.dtype)
    for r in range(N):
        y[r][:, :WIDTHS[r]] = s[:, OFF[r]:OFF[r] + WIDTHS[r]]
    return {"y": y}

@@ -1,0 +1,140 @@
+from concourse.bass import DstId, RemoteDMATransfer
+
+NCHIP = 8
+RK = 2
+SLOT = 64
+C_ALL = 312
+
+SCRATCH = {
+    "xs": ("sbuf", [128, C_ALL], "float32"),
+    "land": ("sbuf", [128, 8 * SLOT], "float32"),
+    "res": ("sbuf", [128, 128], "float32"),
+}
+SEMAPHORES = ["ld0", "ld1", "st", "sent", "arr", "fin"]
+
+BLOCKS = {
+    0: ("H", [(0, 64, 3), (64, 64, 6)]),
+    4: ("H", [(0, 32, 1), (32, 32, 5)]),
+    2: ("H", [(0, 20, 0), (20, 20, 4)]),
+    6: ("D", [(0, 4, 7)]),
+    1: ("D", [(0, 8, 3)]),
+    3: ("D", [(0, 16, 3)]),
+    5: ("D", [(0, 24, 3)]),
+    7: ("D", [(0, 28, 3)]),
+}
+CALLS = [
+    [(0, 0, 4), (0, 1, 4)],
+    [(7, 0, 2), (5, 0, 2), (3, 0, 2), (1, 0, 2)],
+    [(4, 0, 4), (4, 1, 4)],
+    [(2, 0, 2), (2, 1, 2), (6, 0, 2)],
+]
+NFIRST = 1
+
+
+def pieces(off):
+    info = {}
+    for group in CALLS:
+        pw = max(BLOCKS[b][1][p][1] for (b, p, e) in group)
+        for (b, p, e) in group:
+            mode, parts = BLOCKS[b]
+            o, w, k = parts[p]
+            lo = off[b] + o
+            s = min(lo, C_ALL - pw)
+            info[(b, p)] = (mode, o, w, k, pw, s, lo - s)
+    return info
+
+
+def stage1(c, info):
+    calls = []
+    for group in CALLS:
+        trs = []
+        lo_bit, hi_bit = 0, 8
+        for (b, p, e) in group:
+            mode, o, w, k, pw, s, uo = info[(b, p)]
+            if mode == "D":
+                t, slot = b, c
+            else:
+                t = c if (c & 1) == (b & 1) else c ^ 1
+                slot = 0 if t == c else 1
+            if t == c and hi_bit + e <= 16:
+                m = ((1 << e) - 1) << hi_bit
+                hi_bit += e
+            else:
+                m = ((1 << e) - 1) << lo_bit
+                lo_bit += e
+            trs.append((8 * t + k, s, pw, slot, m, e))
+        assert lo_bit <= 8
+        calls.append(trs)
+    return calls
+
+
+def dst_id(topo, core):
+    rid, pid, se = topo.addr(core)
+    return DstId(rid=rid, pnc=pid)
+
+
+def rank_core(g, core, T, topo, info):
+    c = core // 8
+    w_own = T.tables["WIDTHS"][c]
+    first = max(tr[1] + tr[2] for call in stage1(c, info)[:NFIRST] for tr in call)
+    g.dma_start(out=T.xs[:, 0:first], in_=T.x[:, 0:first]).then_inc(T.sem.ld0, 16)
+    g.dma_start(out=T.xs[:, first:C_ALL], in_=T.x[:, first:C_ALL]).then_inc(T.sem.ld1, 16)
+    sent = 0
+    for i, call in enumerate(stage1(c, info)):
+        if i == 0:
+            g.wait_ge(T.sem.ld0, 16)
+        if i == NFIRST:
+            g.wait_ge(T.sem.ld1, 16)
+        trs = []
+        for (dst, s, pw, slot, m, e) in call:
+            trs.append(RemoteDMATransfer(
+                dst_ids=[dst_id(topo, dst)], dma_engine_mask=m, remote_sem=T.sem.arr,
+                srcs=[T.xs[:, s:s + pw]], dsts=[T.land[:, slot * SLOT:slot * SLOT + pw]], alu_op=0))
+            sent += e
+        g.remote_dma_fused(trs, local_sem=T.sem.sent)
+    g.wait_ge(T.sem.fin, 16 * len(BLOCKS[c][1]))
+    g.dma_start(out=T.y[:, 0:w_own], in_=T.res[:, 0:w_own]).then_inc(T.sem.st, 16)
+    g.wait_ge(T.sem.sent, sent)
+    g.wait_ge(T.sem.st, 16)
+
+
+def helper_core(g, core, T, topo, info):
+    c, k = divmod(core, 8)
+    role = None
+    for (b, p), v in info.items():
+        if v[3] == k and ((v[0] == "D" and b == c) or (v[0] == "H" and (b & 1) == (c & 1))):
+            assert role is None
+            role = (b, p)
+    if role is None:
+        return
+    b, p = role
+    mode, o, w, k, pw, s, uo = info[role]
+    n = sum(tr[5] for cc in range(NCHIP) for call in stage1(cc, info) for tr in call if tr[0] == core)
+    if mode == "D":
+        slots = list(range(NCHIP))
+    else:
+        slots = [0, 1]
+        if b == c:
+            slots += [2 + t // 2 for t in range(b & 1, NCHIP, 2) if t != b]
+            n += 8 * 3
+    g.wait_ge(T.sem.arr, n)
+    srcs = [T.land[:, q * SLOT + uo:q * SLOT + uo + w] for q in slots]
+    if b == c:
+        tr = RemoteDMATransfer(dst_ids=[dst_id(topo, 8 * c + RK)], dma_engine_mask=0xFFFF, remote_sem=T.sem.fin,
+                               srcs=srcs, dsts=[T.res[:, o:o + w]], alu_op=1)
+        e = 16
+    else:
+        q = 2 + c // 2
+        tr = RemoteDMATransfer(dst_ids=[dst_id(topo, 8 * b + k)], dma_engine_mask=0x00FF, remote_sem=T.sem.arr,
+                               srcs=srcs, dsts=[T.land[:, q * SLOT + uo:q * SLOT + uo + w]], alu_op=1)
+        e = 8
+    g.remote_dma_fused([tr], local_sem=T.sem.sent)
+    g.wait_ge(T.sem.sent, e)
+
+
+def rank_program(g, core, T, topo):
+    info = pieces(T.tables["OFF"])
+    if T.rank_of(core) is not None:
+        rank_core(g, core, T, topo, info)
+    else:
+        helper_core(g, core, T, topo, info)

@@ -14,8 +14,8 @@ SEMAPHORES = ["ld0", "ld1", "st", "sent", "arr", "fin"]
 
 BLOCKS = {
     0: ("H", [(0, 64, 3), (64, 64, 6)]),
-    4: ("H", [(0, 32, 1), (32, 32, 5)]),
-    2: ("H", [(0, 20, 0), (20, 20, 4)]),
+    4: ("H", [(0, 64, 5)]),
+    2: ("H", [(0, 40, 0)]),
     6: ("D", [(0, 4, 7)]),
     1: ("D", [(0, 8, 3)]),
     3: ("D", [(0, 16, 3)]),
@@ -23,12 +23,10 @@ BLOCKS = {
     7: ("D", [(0, 28, 3)]),
 }
 CALLS = [
-    [(0, 0, 4), (0, 1, 4)],
-    [(7, 0, 2), (5, 0, 2), (3, 0, 2), (1, 0, 2)],
-    [(4, 0, 4), (4, 1, 4)],
-    [(2, 0, 2), (2, 1, 2), (6, 0, 2)],
+    [(0, 0, 2), (0, 1, 2), (4, 0, 2), (2, 0, 2)],
+    [(7, 0, 2), (5, 0, 2), (3, 0, 2), (1, 0, 1), (6, 0, 1)],
 ]
-NFIRST = 1
+NFIRST = 0
 
 
 def pieces(off):
@@ -76,12 +74,13 @@ def dst_id(topo, core):
 def rank_core(g, core, T, topo, info):
     c = core // 8
     w_own = T.tables["WIDTHS"][c]
-    first = max(tr[1] + tr[2] for call in stage1(c, info)[:NFIRST] for tr in call)
-    g.dma_start(out=T.xs[:, 0:first], in_=T.x[:, 0:first]).then_inc(T.sem.ld0, 16)
+    first = max([0] + [tr[1] + tr[2] for call in stage1(c, info)[:NFIRST] for tr in call])
+    if first:
+        g.dma_start(out=T.xs[:, 0:first], in_=T.x[:, 0:first]).then_inc(T.sem.ld0, 16)
     g.dma_start(out=T.xs[:, first:C_ALL], in_=T.x[:, first:C_ALL]).then_inc(T.sem.ld1, 16)
     sent = 0
     for i, call in enumerate(stage1(c, info)):
-        if i == 0:
+        if i == 0 and first:
             g.wait_ge(T.sem.ld0, 16)
         if i == NFIRST:
             g.wait_ge(T.sem.ld1, 16)

@@ -2,15 +2,18 @@ from concourse.bass import DstId, RemoteDMATransfer
 
 NCHIP = 8
 RK = 2
-SLOT = 64
 C_ALL = 312
+WW, WS = 64, 28
 
 SCRATCH = {
     "xs": ("sbuf", [128, C_ALL], "float32"),
-    "land": ("sbuf", [128, 8 * SLOT], "float32"),
-    "res": ("sbuf", [128, 128], "float32"),
+    "landw": ("dram", [8, 128, WW], "float32"),
+    "lands": ("dram", [8, 128, WS], "float32"),
+    "resw": ("dram", [1, 128, WW], "float32"),
+    "ress": ("dram", [128, WS], "float32"),
+    "resb": ("sbuf", [128, 128], "float32"),
 }
-SEMAPHORES = ["ld0", "ld1", "st", "sent", "arr", "fin"]
+SEMAPHORES = ["ld", "st", "sent", "arr", "fin"]
 
 BLOCKS = {
     0: ("H", [(0, 64, 3), (64, 64, 6)]),
@@ -26,19 +29,19 @@ CALLS = [
     [(0, 0, 2), (0, 1, 2), (4, 0, 2), (2, 0, 2)],
     [(7, 0, 2), (5, 0, 2), (3, 0, 2), (1, 0, 1), (6, 0, 1)],
 ]
-NFIRST = 0
 
 
 def pieces(off):
     info = {}
-    for group in CALLS:
-        pw = max(BLOCKS[b][1][p][1] for (b, p, e) in group)
+    for ci, group in enumerate(CALLS):
+        pw = (WW, WS)[ci]
         for (b, p, e) in group:
             mode, parts = BLOCKS[b]
             o, w, k = parts[p]
+            assert w <= pw
             lo = off[b] + o
             s = min(lo, C_ALL - pw)
-            info[(b, p)] = (mode, o, w, k, pw, s, lo - s)
+            info[(b, p)] = (mode, o, w, k, ci, s, lo - s)
     return info
 
 
@@ -48,7 +51,7 @@ def stage1(c, info):
         trs = []
         lo_bit, hi_bit = 0, 8
         for (b, p, e) in group:
-            mode, o, w, k, pw, s, uo = info[(b, p)]
+            mode, o, w, k, ci, s, uo = info[(b, p)]
             if mode == "D":
                 t, slot = b, c
             else:
@@ -60,7 +63,7 @@ def stage1(c, info):
             else:
                 m = ((1 << e) - 1) << lo_bit
                 lo_bit += e
-            trs.append((8 * t + k, s, pw, slot, m, e))
+            trs.append((8 * t + k, s, slot, m, e))
         assert lo_bit <= 8
         calls.append(trs)
     return calls
@@ -73,26 +76,28 @@ def dst_id(topo, core):
 
 def rank_core(g, core, T, topo, info):
     c = core // 8
-    w_own = T.tables["WIDTHS"][c]
-    first = max([0] + [tr[1] + tr[2] for call in stage1(c, info)[:NFIRST] for tr in call])
-    if first:
-        g.dma_start(out=T.xs[:, 0:first], in_=T.x[:, 0:first]).then_inc(T.sem.ld0, 16)
-    g.dma_start(out=T.xs[:, first:C_ALL], in_=T.x[:, first:C_ALL]).then_inc(T.sem.ld1, 16)
+    g.dma_start(out=T.xs[:, :], in_=T.x[:, :]).then_inc(T.sem.ld, 16)
+    g.wait_ge(T.sem.ld, 16)
     sent = 0
-    for i, call in enumerate(stage1(c, info)):
-        if i == 0 and first:
-            g.wait_ge(T.sem.ld0, 16)
-        if i == NFIRST:
-            g.wait_ge(T.sem.ld1, 16)
+    for ci, call in enumerate(stage1(c, info)):
+        pw = (WW, WS)[ci]
+        land = (T.landw, T.lands)[ci]
         trs = []
-        for (dst, s, pw, slot, m, e) in call:
+        for (dst, s, slot, m, e) in call:
             trs.append(RemoteDMATransfer(
                 dst_ids=[dst_id(topo, dst)], dma_engine_mask=m, remote_sem=T.sem.arr,
-                srcs=[T.xs[:, s:s + pw]], dsts=[T.land[:, slot * SLOT:slot * SLOT + pw]], alu_op=0))
+                srcs=[T.xs[:, s:s + pw]], dsts=[land[slot]], alu_op=0))
             sent += e
         g.remote_dma_fused(trs, local_sem=T.sem.sent)
-    g.wait_ge(T.sem.fin, 16 * len(BLOCKS[c][1]))
-    g.dma_start(out=T.y[:, 0:w_own], in_=T.res[:, 0:w_own]).then_inc(T.sem.st, 16)
+    parts = BLOCKS[c][1]
+    g.wait_ge(T.sem.fin, 16 * len(parts))
+    w = T.tables["WIDTHS"][c]
+    ci, uo = info[(c, 0)][4], info[(c, 0)][6]
+    if len(parts) > 1:
+        src = T.resb[:, 0:w]
+    else:
+        src = T.resw[0, :, uo:uo + w] if ci == 0 else T.ress[:, uo:uo + w]
+    g.dma_start(out=T.y[:, 0:w], in_=src).then_inc(T.sem.st, 16)
     g.wait_ge(T.sem.sent, sent)
     g.wait_ge(T.sem.st, 16)
 
@@ -107,8 +112,9 @@ def helper_core(g, core, T, topo, info):
     if role is None:
         return
     b, p = role
-    mode, o, w, k, pw, s, uo = info[role]
-    n = sum(tr[5] for cc in range(NCHIP) for call in stage1(cc, info) for tr in call if tr[0] == core)
+    mode, o, w, k, ci, s, uo = info[role]
+    land = (T.landw, T.lands)[ci]
+    n = sum(tr[4] for cc in range(NCHIP) for call in stage1(cc, info) for tr in call if tr[0] == core)
     if mode == "D":
         slots = list(range(NCHIP))
     else:
@@ -117,15 +123,19 @@ def helper_core(g, core, T, topo, info):
             slots += [2 + t // 2 for t in range(b & 1, NCHIP, 2) if t != b]
             n += 8 * 3
     g.wait_ge(T.sem.arr, n)
-    srcs = [T.land[:, q * SLOT + uo:q * SLOT + uo + w] for q in slots]
+    srcs = [land[q] for q in slots]
     if b == c:
+        if len(BLOCKS[b][1]) > 1:
+            assert uo == 0 and w == WW
+            dst = T.resb[:, o:o + w]
+        else:
+            dst = T.resw[0] if ci == 0 else T.ress[:, :]
         tr = RemoteDMATransfer(dst_ids=[dst_id(topo, 8 * c + RK)], dma_engine_mask=0xFFFF, remote_sem=T.sem.fin,
-                               srcs=srcs, dsts=[T.res[:, o:o + w]], alu_op=1)
+                               srcs=srcs, dsts=[dst], alu_op=1)
         e = 16
     else:
-        q = 2 + c // 2
         tr = RemoteDMATransfer(dst_ids=[dst_id(topo, 8 * b + k)], dma_engine_mask=0x00FF, remote_sem=T.sem.arr,
-                               srcs=srcs, dsts=[T.land[:, q * SLOT + uo:q * SLOT + uo + w]], alu_op=1)
+                               srcs=srcs, dsts=[land[2 + c // 2]], alu_op=1)
         e = 8
     g.remote_dma_fused([tr], local_sem=T.sem.sent)
     g.wait_ge(T.sem.sent, e)

@@ -3,7 +3,7 @@ from concourse.bass import DstId, RemoteDMATransfer
 NCHIP = 8
 RK = 2
 C_ALL = 312
-WW, WS = 64, 28
+WW, WS = 64, 32
 
 SCRATCH = {
     "xs": ("sbuf", [128, C_ALL], "float32"),
@@ -19,15 +19,15 @@ BLOCKS = {
     0: ("H", [(0, 64, 3), (64, 64, 6)]),
     4: ("H", [(0, 64, 5)]),
     2: ("H", [(0, 40, 0)]),
-    6: ("D", [(0, 4, 7)]),
     1: ("D", [(0, 8, 3)]),
     3: ("D", [(0, 16, 3)]),
     5: ("D", [(0, 24, 3)]),
     7: ("D", [(0, 28, 3)]),
 }
+RIDE = {6: 7}
 CALLS = [
     [(0, 0, 2), (0, 1, 2), (4, 0, 2), (2, 0, 2)],
-    [(7, 0, 2), (5, 0, 2), (3, 0, 2), (1, 0, 1), (6, 0, 1)],
+    [(7, 0, 2), (5, 0, 2), (3, 0, 2), (1, 0, 2)],
 ]
 
 
@@ -69,6 +69,10 @@ def stage1(c, info):
     return calls
 
 
+def last_engines(b):
+    return (8, 0x00FF) if b in RIDE.values() else (16, 0xFFFF)
+
+
 def dst_id(topo, core):
     rid, pid, se = topo.addr(core)
     return DstId(rid=rid, pnc=pid)
@@ -89,10 +93,12 @@ def rank_core(g, core, T, topo, info):
                 srcs=[T.xs[:, s:s + pw]], dsts=[land[slot]], alu_op=0))
             sent += e
         g.remote_dma_fused(trs, local_sem=T.sem.sent)
-    parts = BLOCKS[c][1]
-    g.wait_ge(T.sem.fin, 16 * len(parts))
+    b = RIDE.get(c, c)
+    parts = BLOCKS[b][1]
+    g.wait_ge(T.sem.fin, last_engines(b)[0] * len(parts))
     w = T.tables["WIDTHS"][c]
-    ci, uo = info[(c, 0)][4], info[(c, 0)][6]
+    ci = info[(b, 0)][4]
+    uo = T.tables["OFF"][c] - info[(b, 0)][5]
     if len(parts) > 1:
         src = T.resb[:, 0:w]
     else:
@@ -130,9 +136,10 @@ def helper_core(g, core, T, topo, info):
             dst = T.resb[:, o:o + w]
         else:
             dst = T.resw[0] if ci == 0 else T.ress[:, :]
-        tr = RemoteDMATransfer(dst_ids=[dst_id(topo, 8 * c + RK)], dma_engine_mask=0xFFFF, remote_sem=T.sem.fin,
-                               srcs=srcs, dsts=[dst], alu_op=1)
-        e = 16
+        to = [b] + [r for r in RIDE if RIDE[r] == b]
+        e, m = last_engines(b)
+        tr = RemoteDMATransfer(dst_ids=[dst_id(topo, 8 * r + RK) for r in to], dma_engine_mask=m,
+                               remote_sem=T.sem.fin, srcs=srcs, dsts=[dst for r in to], alu_op=1)
     else:
         tr = RemoteDMATransfer(dst_ids=[dst_id(topo, 8 * b + k)], dma_engine_mask=0x00FF, remote_sem=T.sem.arr,
                                srcs=srcs, dsts=[land[2 + c // 2]], alu_op=1)

@@ -16,17 +16,18 @@ SCRATCH = {
 SEMAPHORES = ["ld", "st", "sent", "arr", "fin"]
 
 BLOCKS = {
-    0: ("H", [(0, 64, 3), (64, 64, 6)]),
-    4: ("H", [(0, 64, 5)]),
-    2: ("H", [(0, 40, 0)]),
-    1: ("D", [(0, 8, 3)]),
-    3: ("D", [(0, 16, 3)]),
-    5: ("D", [(0, 24, 3)]),
-    7: ("D", [(0, 28, 3)]),
+    0: ("H", [(0, 64, 3, 3), (64, 64, 6, 6)]),
+    4: ("H", [(0, 64, 5, 6)]),
+    2: ("H", [(0, 40, 0, 7)]),
+    1: ("D", [(0, 8, 3, 3)]),
+    3: ("D", [(0, 16, 3, 3)]),
+    5: ("D", [(0, 24, 3, 3)]),
+    7: ("D", [(0, 28, 3, 3)]),
 }
+FOLD_PARITY = {0: 0, 4: 1, 2: 1}
 RIDE = {6: 7}
 CALLS = [
-    [(0, 0, 2), (0, 1, 2), (4, 0, 2), (2, 0, 2)],
+    [(0, 0, 4), (0, 1, 4), (4, 0, 4), (2, 0, 4)],
     [(7, 0, 2), (5, 0, 2), (3, 0, 2), (1, 0, 2)],
 ]
 
@@ -37,11 +38,11 @@ def pieces(off):
         pw = (WW, WS)[ci]
         for (b, p, e) in group:
             mode, parts = BLOCKS[b]
-            o, w, k = parts[p]
+            o, w, k, kp = parts[p]
             assert w <= pw
             lo = off[b] + o
             s = min(lo, C_ALL - pw)
-            info[(b, p)] = (mode, o, w, k, ci, s, lo - s)
+            info[(b, p)] = (mode, o, w, k, ci, s, lo - s, kp)
     return info
 
 
@@ -51,11 +52,11 @@ def stage1(c, info):
         trs = []
         lo_bit, hi_bit = 0, 8
         for (b, p, e) in group:
-            mode, o, w, k, ci, s, uo = info[(b, p)]
+            mode, o, w, k, ci, s, uo, kp = info[(b, p)]
             if mode == "D":
                 t, slot = b, c
             else:
-                t = c if (c & 1) == (b & 1) else c ^ 1
+                t = c if (c & 1) == FOLD_PARITY[b] else c ^ 1
                 slot = 0 if t == c else 1
             if t == c and hi_bit + e <= 16:
                 m = ((1 << e) - 1) << hi_bit
@@ -63,7 +64,7 @@ def stage1(c, info):
             else:
                 m = ((1 << e) - 1) << lo_bit
                 lo_bit += e
-            trs.append((8 * t + k, s, slot, m, e))
+            trs.append((8 * t + kp, s, slot, m, e))
         assert lo_bit <= 8
         calls.append(trs)
     return calls
@@ -109,28 +110,31 @@ def rank_core(g, core, T, topo, info):
 
 
 def helper_core(g, core, T, topo, info):
-    c, k = divmod(core, 8)
+    c, kk = divmod(core, 8)
     role = None
     for (b, p), v in info.items():
-        if v[3] == k and ((v[0] == "D" and b == c) or (v[0] == "H" and (b & 1) == (c & 1))):
+        pair = v[0] == "H" and (c & 1) == FOLD_PARITY[b] and v[7] == kk
+        last = b == c and v[3] == kk
+        if pair or last:
             assert role is None
-            role = (b, p)
+            role = (b, p, pair, last)
     if role is None:
         return
-    b, p = role
-    mode, o, w, k, ci, s, uo = info[role]
+    b, p, pair, last = role
+    mode, o, w, k, ci, s, uo, kp = info[(b, p)]
     land = (T.landw, T.lands)[ci]
     n = sum(tr[4] for cc in range(NCHIP) for call in stage1(cc, info) for tr in call if tr[0] == core)
     if mode == "D":
         slots = list(range(NCHIP))
     else:
-        slots = [0, 1]
-        if b == c:
-            slots += [2 + t // 2 for t in range(b & 1, NCHIP, 2) if t != b]
-            n += 8 * 3
+        slots = [0, 1] if pair else []
+        if last:
+            more = [2 + t // 2 for t in range(FOLD_PARITY[b], NCHIP, 2) if t != c]
+            slots += more
+            n += 8 * len(more)
     g.wait_ge(T.sem.arr, n)
     srcs = [land[q] for q in slots]
-    if b == c:
+    if last:
         if len(BLOCKS[b][1]) > 1:
             assert uo == 0 and w == WW
             dst = T.resb[:, o:o + w]

from concourse.bass import DstId, RemoteDMATransfer

NCHIP = 8
RK = 2
C_ALL = 312
WW, WS = 64, 32

SCRATCH = {
    "xs": ("sbuf", [128, C_ALL], "float32"),
    "landw": ("dram", [8, 128, WW], "float32"),
    "lands": ("dram", [8, 128, WS], "float32"),
    "resw": ("dram", [1, 128, WW], "float32"),
    "ress": ("dram", [128, WS], "float32"),
    "resb": ("sbuf", [128, 128], "float32"),
}
SEMAPHORES = ["ld", "st", "sent", "arr", "fin"]

BLOCKS = {
    0: ("H", [(0, 64, 3, 3), (64, 64, 6, 6)]),
    4: ("H", [(0, 64, 5, 6)]),
    2: ("H", [(0, 40, 0, 7)]),
    1: ("D", [(0, 8, 3, 3)]),
    3: ("D", [(0, 16, 3, 3)]),
    5: ("D", [(0, 24, 3, 3)]),
    7: ("D", [(0, 28, 3, 3)]),
}
FOLD_PARITY = {0: 0, 4: 1, 2: 1}
RIDE = {6: 7}
CALLS = [
    [(0, 0, 4), (0, 1, 4), (4, 0, 4), (2, 0, 4)],
    [(7, 0, 2), (5, 0, 2), (3, 0, 2), (1, 0, 2)],
]


def pieces(off):
    info = {}
    for ci, group in enumerate(CALLS):
        pw = (WW, WS)[ci]
        for (b, p, e) in group:
            mode, parts = BLOCKS[b]
            o, w, k, kp = parts[p]
            assert w <= pw
            lo = off[b] + o
            s = min(lo, C_ALL - pw)
            info[(b, p)] = (mode, o, w, k, ci, s, lo - s, kp)
    return info


def stage1(c, info):
    calls = []
    for group in CALLS:
        trs = []
        lo_bit, hi_bit = 0, 8
        for (b, p, e) in group:
            mode, o, w, k, ci, s, uo, kp = info[(b, p)]
            if mode == "D":
                t, slot = b, c
            else:
                t = c if (c & 1) == FOLD_PARITY[b] else c ^ 1
                slot = 0 if t == c else 1
            if t == c and hi_bit + e <= 16:
                m = ((1 << e) - 1) << hi_bit
                hi_bit += e
            else:
                m = ((1 << e) - 1) << lo_bit
                lo_bit += e
            trs.append((8 * t + kp, s, slot, m, e))
        assert lo_bit <= 8
        calls.append(trs)
    return calls


def last_engines(b):
    return (8, 0x00FF) if b in RIDE.values() else (16, 0xFFFF)


def dst_id(topo, core):
    rid, pid, se = topo.addr(core)
    return DstId(rid=rid, pnc=pid)


def rank_core(g, core, T, topo, info):
    c = core // 8
    g.dma_start(out=T.xs[:, :], in_=T.x[:, :]).then_inc(T.sem.ld, 16)
    g.wait_ge(T.sem.ld, 16)
    sent = 0
    for ci, call in enumerate(stage1(c, info)):
        pw = (WW, WS)[ci]
        land = (T.landw, T.lands)[ci]
        trs = []
        for (dst, s, slot, m, e) in call:
            trs.append(RemoteDMATransfer(
                dst_ids=[dst_id(topo, dst)], dma_engine_mask=m, remote_sem=T.sem.arr,
                srcs=[T.xs[:, s:s + pw]], dsts=[land[slot]], alu_op=0))
            sent += e
        g.remote_dma_fused(trs, local_sem=T.sem.sent)
    b = RIDE.get(c, c)
    parts = BLOCKS[b][1]
    g.wait_ge(T.sem.fin, last_engines(b)[0] * len(parts))
    w = T.tables["WIDTHS"][c]
    ci = info[(b, 0)][4]
    uo = T.tables["OFF"][c] - info[(b, 0)][5]
    if len(parts) > 1:
        src = T.resb[:, 0:w]
    else:
        src = T.resw[0, :, uo:uo + w] if ci == 0 else T.ress[:, uo:uo + w]
    g.dma_start(out=T.y[:, 0:w], in_=src).then_inc(T.sem.st, 16)
    g.wait_ge(T.sem.sent, sent)
    g.wait_ge(T.sem.st, 16)


def helper_core(g, core, T, topo, info):
    c, kk = divmod(core, 8)
    role = None
    for (b, p), v in info.items():
        pair = v[0] == "H" and (c & 1) == FOLD_PARITY[b] and v[7] == kk
        last = b == c and v[3] == kk
        if pair or last:
            assert role is None
            role = (b, p, pair, last)
    if role is None:
        return
    b, p, pair, last = role
    mode, o, w, k, ci, s, uo, kp = info[(b, p)]
    land = (T.landw, T.lands)[ci]
    n = sum(tr[4] for cc in range(NCHIP) for call in stage1(cc, info) for tr in call if tr[0] == core)
    if mode == "D":
        slots = list(range(NCHIP))
    else:
        slots = [0, 1] if pair else []
        if last:
            more = [2 + t // 2 for t in range(FOLD_PARITY[b], NCHIP, 2) if t != c]
            slots += more
            n += 8 * len(more)
    g.wait_ge(T.sem.arr, n)
    srcs = [land[q] for q in slots]
    if last:
        if len(BLOCKS[b][1]) > 1:
            assert uo == 0 and w == WW
            dst = T.resb[:, o:o + w]
        else:
            dst = T.resw[0] if ci == 0 else T.ress[:, :]
        to = [b] + [r for r in RIDE if RIDE[r] == b]
        e, m = last_engines(b)
        tr = RemoteDMATransfer(dst_ids=[dst_id(topo, 8 * r + RK) for r in to], dma_engine_mask=m,
                               remote_sem=T.sem.fin, srcs=srcs, dsts=[dst for r in to], alu_op=1)
    else:
        tr = RemoteDMATransfer(dst_ids=[dst_id(topo, 8 * b + k)], dma_engine_mask=0x00FF, remote_sem=T.sem.arr,
                               srcs=srcs, dsts=[land[2 + c // 2]], alu_op=1)
        e = 8
    g.remote_dma_fused([tr], local_sem=T.sem.sent)
    g.wait_ge(T.sem.sent, e)


def rank_program(g, core, T, topo):
    info = pieces(T.tables["OFF"])
    if T.rank_of(core) is not None:
        rank_core(g, core, T, topo, info)
    else:
        helper_core(g, core, T, topo, info)
